import numpy as np
import ml_dtypes


def mxq(x, axis, fmt="e4m3"):
    dtype, down = {"e4m3": (ml_dtypes.float8_e4m3fn, 7), "e5m2": (ml_dtypes.float8_e5m2, 14)}[fmt]
    v = np.moveaxis(np.asarray(x, np.float32).astype(ml_dtypes.bfloat16).astype(np.float64), axis, -1)
    blocks = v.reshape(v.shape[:-1] + (-1, 32))
    amax = np.abs(blocks).max(-1, keepdims=True)
    byte = np.maximum(np.where(amax > 0, np.frexp(amax)[1] - 1 + 127, 0) - down, 1)
    scale = np.exp2(byte - 127.0)
    codes = (blocks / scale).astype(np.float32).astype(dtype).astype(np.float64)
    return np.moveaxis((codes * scale).reshape(v.shape), -1, axis)


WIDE = False


def mx_kscale(k):
    if not WIDE:
        return np.ones(k)
    levels = np.array([10, -10, 5, -5, 0])
    if k % 512:
        return np.exp2(np.random.permutation(np.resize(levels, k // 32))).repeat(32)
    a = np.empty((k // 512, 16))
    for p in range(k // 512):
        a[p, :8] = np.random.permutation(np.resize(levels, 8))
        for g in range(8):
            far = levels[np.abs(levels - a[p, g]) >= 10]
            a[p, g + 8] = far[np.random.randint(len(far))]
    return np.exp2(a.ravel()).repeat(32)


def f64(x):
    return np.asarray(x).astype(np.float64)


def striped8(idx):
    return np.concatenate([x.reshape(-1, 16).T for x in idx]).astype(np.uint16)


def runs(offs, k):
    lists = np.stack([offs[16 * r : 16 * r + 16].T.reshape(-1) for r in range(8)]).astype(np.int64)
    return lists[np.arange(k) % 512 // 64]


def pack_weight(w):
    k, n = w.shape
    w = f64(np.asarray(w, np.float32).astype(ml_dtypes.bfloat16)).reshape(k // 32, 32, n)
    amax = np.abs(w).max(1)
    byte = np.clip(np.where(amax > 0, np.frexp(amax)[1] - 1 + 127 - 7, 1), 1, 254)
    scaled = (w * np.exp2(127.0 - byte)[:, None, :]).reshape(k, n).astype(np.float32)
    words = np.ascontiguousarray(scaled.reshape(k // 512, 128, 4, n).transpose(0, 1, 3, 2)).astype(ml_dtypes.float8_e4m3fn).view(np.uint8)
    return words, np.ascontiguousarray(byte.astype(np.uint8).reshape(k // 512, 16, n))


def unpack_weight(words, scales):
    g, p, n, _ = words.shape
    vals = np.ascontiguousarray(words).view(ml_dtypes.float8_e4m3fn).astype(np.float64) * np.repeat(np.exp2(scales.astype(np.float64) - 127.0), 8, axis=1)[..., None]
    return vals.transpose(0, 1, 3, 2).reshape(g * 512, n)


E2M1 = np.array([0.0, 0.5, 1.0, 1.5, 2.0, 3.0, 4.0, 6.0, -0.0, -0.5, -1.0, -1.5, -2.0, -3.0, -4.0, -6.0])


def pack_fp4(w):
    k, n = w.shape
    w = f64(np.asarray(w, np.float32).astype(ml_dtypes.bfloat16)).reshape(k // 32, 32, n)
    amax = np.abs(w).max(1)
    mant, ex = np.frexp(amax / 6.0)
    byte = np.clip(np.where(amax > 0, np.where(mant > 0.5, ex, ex - 1) + 127, 1), 1, 254)
    scaled = (w * np.exp2(127.0 - byte)[:, None, :]).reshape(k, n).astype(np.float32)
    c = np.ascontiguousarray(scaled.reshape(k // 512, 128, 4, n).transpose(0, 1, 3, 2)).astype(ml_dtypes.float4_e2m1fn).view(np.uint8) & 0xF
    words = (c[..., 0::2] | (c[..., 1::2] << 4)).reshape(k // 512, 128, 2 * n)
    return np.ascontiguousarray(words), np.ascontiguousarray(byte.astype(np.uint8).reshape(k // 512, 16, n))


def unpack_fp4(words, scales):
    g, _, n = scales.shape
    words = np.ascontiguousarray(words).reshape(g, 128, n, 2)
    nib = np.empty((g, 128, n, 4), np.uint8)
    nib[..., 0::2] = words & 0xF
    nib[..., 1::2] = words >> 4
    vals = E2M1[nib] * np.repeat(np.exp2(scales.astype(np.float64) - 127.0), 8, axis=1)[..., None]
    return vals.transpose(0, 1, 3, 2).reshape(g * 512, n)


def sigmoid(v):
    return 1.0 / (1.0 + np.exp(-np.maximum(v, -700.0)))

def planes(y):
    n, m = y.shape
    v = y.astype(np.float32).astype(ml_dtypes.bfloat16).astype(np.float64).reshape(n // 32, 32, m)
    top = np.abs(v).max(1)
    byte = np.clip(np.where(top > 0, np.frexp(top)[1] - 1 + 127 - 7, 1), 1, 254)
    codes = (v * np.exp2(127.0 - byte)[:, None, :]).reshape(n, m).astype(np.float32).astype(ml_dtypes.float8_e4m3fn).view(np.uint8)
    words = codes.reshape(n // 512, 128, 4, m).transpose(0, 1, 3, 2)
    return np.ascontiguousarray(words), np.ascontiguousarray(byte.astype(np.uint8).reshape(n // 512, 16, m))


K, T, S, H, U, C = 512, 2048, 512, 512, 1024, 512


def setup_inputs():
    n = np.random.standard_normal
    s = mx_kscale(K)[:, None]
    packed_xT = pack_weight(n((K, T)) * s)
    packed_w1 = pack_fp4(n((K, H)) / np.sqrt(K) / s)
    return {
        "x_words": packed_xT[0],
        "x_scales": packed_xT[1],
        "w1_words": packed_w1[0],
        "w1_scales": packed_w1[1],
        "mem": n((H, U)).astype(np.float32),
        "gs": (np.random.uniform(0.5, 1.5, (K, 1)) / s).astype(np.float32),
        "offs": striped8(np.random.randint(0, T, (8, S))),
        "n1": striped8(np.stack([np.random.permutation(U)[:S] for _ in range(8)])),
        "cand": striped8(np.random.randint(0, T, (8, C))),
        "n2": striped8(np.stack([np.random.permutation(U) for _ in range(8)])),
        "n3": striped8(np.stack([np.random.permutation(U) for _ in range(8)])),
    }


def reference(x_words, x_scales, w1_words, w1_scales, mem, gs, offs, n1, cand, n2, n3):
    x_cand = unpack_weight(x_words, x_scales)[np.arange(K)[:, None], runs(cand, K)]
    old = f64(mem)[np.arange(H)[:, None], runs(n1, H)]
    xq = unpack_weight(x_words, x_scales)[np.arange(K)[:, None], runs(offs, K)]
    y = unpack_fp4(w1_words, w1_scales).T @ xq
    nw = old + sigmoid(y) * (y - old)
    pg = f64(mem).copy()
    pg[np.arange(H)[:, None], runs(n1, H)] = nw
    z = f64(gs) * pg
    s = 0.0625 * ((x_cand.T @ mxq(z, 0, "e4m3")))
    out_0 = np.maximum(s * (sigmoid(s[np.arange(C)[:, None], runs(n2, C)])), s[np.arange(C)[:, None], runs(n3, C)])
    return (out_0,) + planes(out_0)

@@ -1,0 +1,243 @@
+from contextlib import ExitStack
+
+import concourse.mybir as mybir
+
+F32 = mybir.dt.float32
+BF16 = mybir.dt.bfloat16
+I32 = mybir.dt.int32
+U32 = mybir.dt.uint32
+U16 = mybir.dt.uint16
+U8 = mybir.dt.uint8
+FP8X4 = mybir.dt.float8_e4m3fn_x4
+FP4X4 = mybir.dt.float4_e2m1fn_x4
+ACT = mybir.ActivationFunctionType
+ALU = mybir.AluOpType
+
+P = 128
+PACK = 4
+T, S, U, C = 2048, 512, 1024, 512
+FLOPS = 2 * 512 * 512 * S + 2 * 512 * C * U
+QUARTER = 256
+CHUNKS = (512, 256, 256)
+
+
+def tile_picked_hcandpagetgmax_none_po_kernel(
+    tc, x_words, x_scales, w1_words, w1_scales, mem, gs, offs, n1, cand, n2, n3, out_0, out_1, out_2
+):
+    nc = tc.nc
+    with ExitStack() as ctx:
+        lists = ctx.enter_context(tc.tile_pool(name="lists", bufs=1))
+        keep = ctx.enter_context(tc.tile_pool(name="keep", bufs=1))
+        ring = ctx.enter_context(tc.tile_pool(name="ring", bufs=3))
+        psum = ctx.enter_context(tc.psum_pool(name="psum", bufs=8))
+
+        def load_list(src, name):
+            tile = lists.tile(list(src.shape), U16, name=name)
+            nc.sync.dma_start(tile[:], src)
+            return tile
+
+        def load_scale_rows(queue, src, name):
+            width = src.shape[-1]
+            tile = keep.tile([P, width], U8, name=name, align_bytes=64)
+            rows = src[0].bitcast(I32).unsqueeze(1).to_broadcast([16, 8, width // 4])
+            queue.dma_start(out=tile[:].bitcast(I32), in_=rows)
+            return tile
+
+        def place_scale_rows(queue, tile):
+            for r in range(1, 4):
+                queue.dma_start(out=tile[r:P:32, :].bitcast(I32), in_=tile[8 * r : P : 32, :].bitcast(I32))
+
+        mem_rows = mem.rearrange("(p t) w -> t p w", t=PACK)
+
+        def load_page(t, name):
+            page = keep.tile([P, U], F32, name=name, align_bytes=64)
+            nc.sync.dma_start(out=page[:], in_=mem_rows[t])
+            return page
+
+        offs_t = load_list(offs, "offs_t")
+        w1s_raw = load_scale_rows(nc.scalar, w1_scales, "w1s_raw")
+        xs_table = load_scale_rows(nc.sync, x_scales, "xs_table")
+        w1w_raw = keep.tile([P, 2 * 512], U8, name="w1w_raw", align_bytes=64)
+        nc.sync.dma_start(out=w1w_raw[:].bitcast(I32), in_=w1_words[0].bitcast(I32))
+        n1_t = load_list(n1, "n1_t")
+        n2_t = load_list(n2, "n2_t")
+        xw_table = keep.tile([P, T], I32, name="xw_table", align_bytes=64)
+        nc.sync.dma_start(out=xw_table[:], in_=x_words[0].rearrange("p c r -> p (c r)").bitcast(I32))
+        cand_t = load_list(cand, "cand_t")
+        pages = [load_page(0, "page0"), load_page(1, "page1")]
+        n3_t = load_list(n3, "n3_t")
+
+        y_scales = keep.tile([P, 512 + S], U8, name="y_scales", align_bytes=64)
+        w1s = y_scales[:, :512]
+        xq_s = y_scales[:, 512:]
+        nc.vector.tensor_copy(
+            w1s.rearrange("p (t m) -> p t m", t=PACK),
+            w1s_raw[:].rearrange("p (m t) -> p t m", t=PACK),
+        )
+        xq_s_picked = keep.tile([P, S], U8, name="w1w", align_bytes=64)
+        nc.vector.tensor_copy(xq_s_picked[:], xs_table[:].indirect(offs_t[:]))
+        nc.vector.tensor_copy(xq_s.bitcast(I32), xq_s_picked[:].bitcast(I32))
+        place_scale_rows(nc.scalar, y_scales)
+
+        w1w = keep.tile([P, 2 * 512], U8, name="w1w", align_bytes=64)
+        nc.vector.tensor_copy(
+            w1w[:].rearrange("p (t m b) -> p t m b", t=PACK, b=2),
+            w1w_raw[:].rearrange("p (m t b) -> p t m b", t=PACK, b=2),
+        )
+        pages.append(load_page(2, "w1w_raw"))
+        xq_w = keep.tile([P, S], I32, name="xq_w", align_bytes=64)
+        nc.vector.tensor_copy(xq_w[:].bitcast(U32), xw_table[:].bitcast(U32).indirect(offs_t[:]))
+
+        xc_s_picked = keep.tile([P, C], U8, name="xc_s_picked", align_bytes=64)
+        nc.vector.tensor_copy(xc_s_picked[:], xs_table[:].indirect(cand_t[:]))
+        xc_s = keep.tile([P, C], U8, name="xc_s", align_bytes=64)
+        nc.vector.tensor_copy(
+            xc_s[:].rearrange("p (t m) -> p t m", t=PACK),
+            xc_s_picked[:].rearrange("p (m t) -> p t m", t=PACK),
+        )
+        place_scale_rows(nc.sync, xc_s)
+        gs_t = keep.tile([P, PACK], F32, name="xs_table", align_bytes=64)
+        nc.sync.dma_start(out=gs_t[:], in_=gs.rearrange("(p t) o -> p (t o)", t=PACK))
+
+        ys = []
+        for t in range(PACK):
+            y = psum.tile([P, 512], F32, name="bank")
+            nc.tensor.matmul_mx(
+                out=y[:],
+                lhsT=w1w[:, 256 * t : 256 * (t + 1)].bitcast(FP4X4),
+                lhsT_scale=w1s[:, P * t : P * (t + 1)],
+                rhs=xq_w[:].bitcast(FP8X4),
+                rhs_scale=xq_s,
+                start=True,
+                stop=True,
+            )
+            ys.append(y)
+        pages.append(load_page(3, "w1w"))
+
+        def keep_gate(t):
+            gate = keep.tile([P, S], F32, name=f"gate{t}")
+            nc.scalar.activation(gate[:], ys[t][:], ACT.Sigmoid, scale=-1.0)
+            return gate
+
+        def gated_y(t):
+            silu = keep.tile([P, S], F32, name=f"silu{t}")
+            nc.scalar.activation(silu[:], ys[t][:], ACT.Silu)
+            return silu
+
+        gates = [keep_gate(t) for t in range(PACK - 1)]
+        silus = [gated_y(t) for t in range(PACK)]
+        gates.append(keep_gate(PACK - 1))
+
+        def kept_old(t):
+            kept = keep.tile([P, S], F32, name=f"kept{t}", align_bytes=64)
+            nc.vector.tensor_tensor(kept[:], pages[t][:].indirect(n1_t[:]), gates[t][:], ALU.mult)
+            return kept
+
+        z16 = keep.tile([P, U, PACK], BF16, name="z16", align_bytes=64)
+
+        def write_page(t, kept):
+            nc.vector.tensor_tensor(pages[t][:].indirect(n1_t[:]), kept[:], silus[t][:], ALU.add)
+            for w0 in range(0, U, QUARTER):
+                nc.scalar.activation(
+                    z16[:, w0 : w0 + QUARTER, t], pages[t][:, w0 : w0 + QUARTER], ACT.Copy, scale=gs_t[:, t : t + 1]
+                )
+
+        kepts = [kept_old(t) for t in range(PACK - 1)]
+        for t in range(PACK - 1):
+            write_page(t, kepts[t])
+        write_page(PACK - 1, kept_old(PACK - 1))
+
+        xc_w_picked = keep.tile([P, C], I32, name=f"kept{PACK - 1}", align_bytes=64)
+        nc.vector.tensor_copy(xc_w_picked[:].bitcast(U32), xw_table[:].bitcast(U32).indirect(cand_t[:]))
+        xc_w = keep.tile([P, C], I32, name="xc_w", align_bytes=64)
+        nc.vector.tensor_copy(
+            xc_w[:].rearrange("p (t m) -> p t m", t=PACK),
+            xc_w_picked[:].rearrange("p (m t) -> p t m", t=PACK),
+        )
+
+        z_w = keep.tile([P, U], I32, name="z_w", align_bytes=64)
+        z_s = keep.tile([P, U], U8, name="z_s", align_bytes=64)
+        for w0 in range(0, U, QUARTER):
+            nc.vector.quantize_mx(
+                out=z_w[:, w0 : w0 + QUARTER].bitcast(FP8X4),
+                scales=z_s[:, w0 : w0 + QUARTER],
+                in_=z16[:, w0 : w0 + QUARTER, :].rearrange("p w t -> p (w t)"),
+            )
+
+        def scores(t):
+            s = keep.tile([P, U], F32, name=f"s{t}")
+            pieces = ((0, 512), (512, 256), (768, 256)) if t == 0 else ((0, 512), (512, 512))
+            for w0, n in pieces:
+                acc = psum.tile([P, 512], F32, name="bank")
+                nc.tensor.matmul_mx(
+                    out=acc[:, :n],
+                    lhsT=xc_w[:, P * t : P * (t + 1)].bitcast(FP8X4),
+                    lhsT_scale=xc_s[:, P * t : P * (t + 1)],
+                    rhs=z_w[:, w0 : w0 + n].bitcast(FP8X4),
+                    rhs_scale=z_s[:, w0 : w0 + n],
+                    start=True,
+                    stop=True,
+                )
+                if t == 0 and w0 + n < U:
+                    nc.vector.tensor_scalar(s[:, w0 : w0 + n], acc[:, :n], 0.0625, None, ALU.mult)
+                else:
+                    nc.scalar.activation(s[:, w0 : w0 + n], acc[:, :n], ACT.Copy, scale=0.0625)
+            return s
+
+        out_rows = out_0.rearrange("(p t) w -> p t w", t=PACK)
+        out_words = out_1[0].rearrange("p c r -> p (c r)").bitcast(I32)
+        o_s = keep.tile([P, U], U8, name="o_s", align_bytes=64)
+        starts = [sum(CHUNKS[:c]) for c in range(len(CHUNKS))]
+        steps = [(c, t) for c in range(len(CHUNKS)) for t in range(PACK)]
+        outs = [keep.tile([P, PACK, width], F32, name=f"o{c}") for c, width in enumerate(CHUNKS)]
+        outs16 = [keep.tile([P, width, PACK], BF16, name=f"o16_{c}", align_bytes=64) for c, width in enumerate(CHUNKS)]
+
+        def entries(c):
+            return slice(starts[c] // 16, (starts[c] + CHUNKS[c]) // 16)
+
+        def fetch_other(c, t):
+            other = ring.tile([P, CHUNKS[c]], F32, name="other")
+            nc.vector.tensor_copy(other[:], ss[t][:].indirect(n3_t[:, entries(c)]))
+            return other
+
+        def regroup(c, piece):
+            n = CHUNKS[c] // PACK
+            cols = slice(piece * n, (piece + 1) * n)
+            nc.scalar.copy(outs16[c][:, cols, :], outs[c][:, :, cols].rearrange("p t w -> p w t"))
+
+        def hand_on(c):
+            cols = slice(starts[c], starts[c] + CHUNKS[c])
+            o_w = keep.tile([P, CHUNKS[c]], I32, name=f"o_w{c}", align_bytes=64)
+            nc.vector.quantize_mx(
+                out=o_w[:].bitcast(FP8X4), scales=o_s[:, cols], in_=outs16[c][:].rearrange("p w t -> p (w t)")
+            )
+            nc.sync.dma_start(out=out_words[:, cols], in_=o_w[:])
+
+        ss = [scores(0), scores(1)]
+        other = fetch_other(*steps[0])
+        for i, (c, t) in enumerate(steps):
+            cols = slice(starts[c], starts[c] + CHUNKS[c])
+            sig = ring.tile([P, CHUNKS[c]], F32, name="sig")
+            nc.scalar.activation(sig[:], ss[t][:].indirect(n2_t[:, entries(c)]), ACT.Sigmoid)
+            if len(ss) < PACK:
+                ss.append(scores(len(ss)))
+            if c > 0:
+                regroup(c - 1, t)
+            prod = ring.tile([P, CHUNKS[c]], F32, name="prod")
+            nc.vector.tensor_tensor(prod[:], ss[t][:, cols], sig[:], ALU.mult)
+            next_other = fetch_other(*steps[i + 1]) if i + 1 < len(steps) else None
+            nc.vector.tensor_tensor(outs[c][:, t, :], prod[:], other[:], ALU.max)
+            other = next_other
+            if t == PACK - 1:
+                nc.sync.dma_start(out=out_rows[:, :, cols], in_=outs[c][:])
+            if c > 1 and t == 0:
+                hand_on(c - 2)
+        last = len(CHUNKS) - 1
+        nc.vector.tensor_copy(outs16[last][:], outs[last][:].rearrange("p t w -> p w t"))
+        hand_on(last - 1)
+        hand_on(last)
+
+        out_scale_rows = out_2[0].bitcast(I32)
+        for q in range(4):
+            queue = nc.scalar if q % 2 == 0 else nc.sync
+            queue.dma_start(out=out_scale_rows[4 * q : 4 * q + 4, :], in_=o_s[32 * q : 32 * q + 4, :].bitcast(I32))

@@ -54,9 +54,9 @@ def tile_picked_hcandpagetgmax_none_po_kernel(
             nc.sync.dma_start(out=page[:], in_=mem_rows[t])
             return page
 
-        offs_t = load_list(offs, "offs_t")
-        w1s_raw = load_scale_rows(nc.scalar, w1_scales, "w1s_raw")
         xs_table = load_scale_rows(nc.sync, x_scales, "xs_table")
+        w1s_raw = load_scale_rows(nc.scalar, w1_scales, "w1s_raw")
+        offs_t = load_list(offs, "offs_t")
         w1w_raw = keep.tile([P, 2 * 512], U8, name="w1w_raw", align_bytes=64)
         nc.sync.dma_start(out=w1w_raw[:].bitcast(I32), in_=w1_words[0].bitcast(I32))
         n1_t = load_list(n1, "n1_t")
@@ -64,7 +64,7 @@ def tile_picked_hcandpagetgmax_none_po_kernel(
         xw_table = keep.tile([P, T], I32, name="xw_table", align_bytes=64)
         nc.sync.dma_start(out=xw_table[:], in_=x_words[0].rearrange("p c r -> p (c r)").bitcast(I32))
         cand_t = load_list(cand, "cand_t")
-        pages = [load_page(0, "page0"), load_page(1, "page1")]
+        pages = [load_page(0, "page0")]
         n3_t = load_list(n3, "n3_t")
 
         y_scales = keep.tile([P, 512 + S], U8, name="y_scales", align_bytes=64)
@@ -84,7 +84,7 @@ def tile_picked_hcandpagetgmax_none_po_kernel(
             w1w[:].rearrange("p (t m b) -> p t m b", t=PACK, b=2),
             w1w_raw[:].rearrange("p (m t b) -> p t m b", t=PACK, b=2),
         )
-        pages.append(load_page(2, "w1w_raw"))
+        pages.append(load_page(1, "w1w_raw"))
         xq_w = keep.tile([P, S], I32, name="xq_w", align_bytes=64)
         nc.vector.tensor_copy(xq_w[:].bitcast(U32), xw_table[:].bitcast(U32).indirect(offs_t[:]))
 
@@ -96,7 +96,8 @@ def tile_picked_hcandpagetgmax_none_po_kernel(
             xc_s_picked[:].rearrange("p (m t) -> p t m", t=PACK),
         )
         place_scale_rows(nc.sync, xc_s)
-        gs_t = keep.tile([P, PACK], F32, name="xs_table", align_bytes=64)
+        pages.append(load_page(2, "xs_table"))
+        gs_t = keep.tile([P, PACK], F32, name="xc_s_picked", align_bytes=64)
         nc.sync.dma_start(out=gs_t[:], in_=gs.rearrange("(p t) o -> p (t o)", t=PACK))
 
         ys = []
@@ -133,13 +134,13 @@ def tile_picked_hcandpagetgmax_none_po_kernel(
             nc.vector.tensor_tensor(kept[:], pages[t][:].indirect(n1_t[:]), gates[t][:], ALU.mult)
             return kept
 
-        z16 = keep.tile([P, U, PACK], BF16, name="z16", align_bytes=64)
+        z16 = [keep.tile([P, QUARTER, PACK], BF16, name=f"z16_{v}", align_bytes=64) for v in range(U // QUARTER)]
 
         def write_page(t, kept):
             nc.vector.tensor_tensor(pages[t][:].indirect(n1_t[:]), kept[:], silus[t][:], ALU.add)
             for w0 in range(0, U, QUARTER):
                 nc.scalar.activation(
-                    z16[:, w0 : w0 + QUARTER, t], pages[t][:, w0 : w0 + QUARTER], ACT.Copy, scale=gs_t[:, t : t + 1]
+                    z16[w0 // QUARTER][:, :, t], pages[t][:, w0 : w0 + QUARTER], ACT.Copy, scale=gs_t[:, t : t + 1]
                 )
 
         kepts = [kept_old(t) for t in range(PACK - 1)]
@@ -151,8 +152,8 @@ def tile_picked_hcandpagetgmax_none_po_kernel(
         nc.vector.tensor_copy(xc_w_picked[:].bitcast(U32), xw_table[:].bitcast(U32).indirect(cand_t[:]))
         xc_w = keep.tile([P, C], I32, name="xc_w", align_bytes=64)
         nc.vector.tensor_copy(
-            xc_w[:].rearrange("p (t m) -> p t m", t=PACK),
-            xc_w_picked[:].rearrange("p (m t) -> p t m", t=PACK),
+            xc_w[:].rearrange("p (t g i) -> p g t i", t=PACK, i=4),
+            xc_w_picked[:].rearrange("p (g i t) -> p g t i", t=PACK, i=4),
         )
 
         z_w = keep.tile([P, U], I32, name="z_w", align_bytes=64)
@@ -161,7 +162,7 @@ def tile_picked_hcandpagetgmax_none_po_kernel(
             nc.vector.quantize_mx(
                 out=z_w[:, w0 : w0 + QUARTER].bitcast(FP8X4),
                 scales=z_s[:, w0 : w0 + QUARTER],
-                in_=z16[:, w0 : w0 + QUARTER, :].rearrange("p w t -> p (w t)"),
+                in_=z16[w0 // QUARTER][:].rearrange("p w t -> p (w t)"),
             )
 
         def scores(t):
@@ -203,7 +204,10 @@ def tile_picked_hcandpagetgmax_none_po_kernel(
         def regroup(c, piece):
             n = CHUNKS[c] // PACK
             cols = slice(piece * n, (piece + 1) * n)
-            nc.scalar.copy(outs16[c][:, cols, :], outs[c][:, :, cols].rearrange("p t w -> p w t"))
+            nc.scalar.copy(
+                outs16[c][:, cols, :].rearrange("p (g i) t -> p g t i", i=4),
+                outs[c][:, :, cols].rearrange("p t (g i) -> p g t i", i=4),
+            )
 
         def hand_on(c):
             cols = slice(starts[c], starts[c] + CHUNKS[c])
@@ -233,7 +237,10 @@ def tile_picked_hcandpagetgmax_none_po_kernel(
             if c > 1 and t == 0:
                 hand_on(c - 2)
         last = len(CHUNKS) - 1
-        nc.vector.tensor_copy(outs16[last][:], outs[last][:].rearrange("p t w -> p w t"))
+        nc.vector.tensor_copy(
+            outs16[last][:].rearrange("p (g i) t -> p g t i", i=4),
+            outs[last][:].rearrange("p t (g i) -> p g t i", i=4),
+        )
         hand_on(last - 1)
         hand_on(last)
 

from contextlib import ExitStack

import concourse.mybir as mybir

F32 = mybir.dt.float32
BF16 = mybir.dt.bfloat16
I32 = mybir.dt.int32
U32 = mybir.dt.uint32
U16 = mybir.dt.uint16
U8 = mybir.dt.uint8
FP8X4 = mybir.dt.float8_e4m3fn_x4
FP4X4 = mybir.dt.float4_e2m1fn_x4
ACT = mybir.ActivationFunctionType
ALU = mybir.AluOpType

P = 128
PACK = 4
T, S, U, C = 2048, 512, 1024, 512
FLOPS = 2 * 512 * 512 * S + 2 * 512 * C * U
QUARTER = 256
CHUNKS = (512, 256, 256)


def tile_picked_hcandpagetgmax_none_po_kernel(
    tc, x_words, x_scales, w1_words, w1_scales, mem, gs, offs, n1, cand, n2, n3, out_0, out_1, out_2
):
    nc = tc.nc
    with ExitStack() as ctx:
        lists = ctx.enter_context(tc.tile_pool(name="lists", bufs=1))
        keep = ctx.enter_context(tc.tile_pool(name="keep", bufs=1))
        ring = ctx.enter_context(tc.tile_pool(name="ring", bufs=3))
        psum = ctx.enter_context(tc.psum_pool(name="psum", bufs=8))

        def load_list(src, name):
            tile = lists.tile(list(src.shape), U16, name=name)
            nc.sync.dma_start(tile[:], src)
            return tile

        def load_scale_rows(queue, src, name):
            width = src.shape[-1]
            tile = keep.tile([P, width], U8, name=name, align_bytes=64)
            rows = src[0].bitcast(I32).unsqueeze(1).to_broadcast([16, 8, width // 4])
            queue.dma_start(out=tile[:].bitcast(I32), in_=rows)
            return tile

        def place_scale_rows(queue, tile):
            for r in range(1, 4):
                queue.dma_start(out=tile[r:P:32, :].bitcast(I32), in_=tile[8 * r : P : 32, :].bitcast(I32))

        mem_rows = mem.rearrange("(p t) w -> t p w", t=PACK)

        def load_page(t, name):
            page = keep.tile([P, U], F32, name=name, align_bytes=64)
            nc.sync.dma_start(out=page[:], in_=mem_rows[t])
            return page

        xs_table = load_scale_rows(nc.sync, x_scales, "xs_table")
        w1s_raw = load_scale_rows(nc.scalar, w1_scales, "w1s_raw")
        offs_t = load_list(offs, "offs_t")
        w1w_raw = keep.tile([P, 2 * 512], U8, name="w1w_raw", align_bytes=64)
        nc.sync.dma_start(out=w1w_raw[:].bitcast(I32), in_=w1_words[0].bitcast(I32))
        n1_t = load_list(n1, "n1_t")
        n2_t = load_list(n2, "n2_t")
        xw_table = keep.tile([P, T], I32, name="xw_table", align_bytes=64)
        nc.sync.dma_start(out=xw_table[:], in_=x_words[0].rearrange("p c r -> p (c r)").bitcast(I32))
        cand_t = load_list(cand, "cand_t")
        pages = [load_page(0, "page0")]
        n3_t = load_list(n3, "n3_t")

        y_scales = keep.tile([P, 512 + S], U8, name="y_scales", align_bytes=64)
        w1s = y_scales[:, :512]
        xq_s = y_scales[:, 512:]
        nc.vector.tensor_copy(
            w1s.rearrange("p (t m) -> p t m", t=PACK),
            w1s_raw[:].rearrange("p (m t) -> p t m", t=PACK),
        )
        xq_s_picked = keep.tile([P, S], U8, name="w1w", align_bytes=64)
        nc.vector.tensor_copy(xq_s_picked[:], xs_table[:].indirect(offs_t[:]))
        nc.vector.tensor_copy(xq_s.bitcast(I32), xq_s_picked[:].bitcast(I32))
        place_scale_rows(nc.scalar, y_scales)

        w1w = keep.tile([P, 2 * 512], U8, name="w1w", align_bytes=64)
        nc.vector.tensor_copy(
            w1w[:].rearrange("p (t m b) -> p t m b", t=PACK, b=2),
            w1w_raw[:].rearrange("p (m t b) -> p t m b", t=PACK, b=2),
        )
        pages.append(load_page(1, "w1w_raw"))
        xq_w = keep.tile([P, S], I32, name="xq_w", align_bytes=64)
        nc.vector.tensor_copy(xq_w[:].bitcast(U32), xw_table[:].bitcast(U32).indirect(offs_t[:]))

        xc_s_picked = keep.tile([P, C], U8, name="xc_s_picked", align_bytes=64)
        nc.vector.tensor_copy(xc_s_picked[:], xs_table[:].indirect(cand_t[:]))
        xc_s = keep.tile([P, C], U8, name="xc_s", align_bytes=64)
        nc.vector.tensor_copy(
            xc_s[:].rearrange("p (t m) -> p t m", t=PACK),
            xc_s_picked[:].rearrange("p (m t) -> p t m", t=PACK),
        )
        place_scale_rows(nc.sync, xc_s)
        pages.append(load_page(2, "xs_table"))
        gs_t = keep.tile([P, PACK], F32, name="xc_s_picked", align_bytes=64)
        nc.sync.dma_start(out=gs_t[:], in_=gs.rearrange("(p t) o -> p (t o)", t=PACK))

        ys = []
        for t in range(PACK):
            y = psum.tile([P, 512], F32, name="bank")
            nc.tensor.matmul_mx(
                out=y[:],
                lhsT=w1w[:, 256 * t : 256 * (t + 1)].bitcast(FP4X4),
                lhsT_scale=w1s[:, P * t : P * (t + 1)],
                rhs=xq_w[:].bitcast(FP8X4),
                rhs_scale=xq_s,
                start=True,
                stop=True,
            )
            ys.append(y)
        pages.append(load_page(3, "w1w"))

        def keep_gate(t):
            gate = keep.tile([P, S], F32, name=f"gate{t}")
            nc.scalar.activation(gate[:], ys[t][:], ACT.Sigmoid, scale=-1.0)
            return gate

        def gated_y(t):
            silu = keep.tile([P, S], F32, name=f"silu{t}")
            nc.scalar.activation(silu[:], ys[t][:], ACT.Silu)
            return silu

        gates = [keep_gate(t) for t in range(PACK - 1)]
        silus = [gated_y(t) for t in range(PACK)]
        gates.append(keep_gate(PACK - 1))

        def kept_old(t):
            kept = keep.tile([P, S], F32, name=f"kept{t}", align_bytes=64)
            nc.vector.tensor_tensor(kept[:], pages[t][:].indirect(n1_t[:]), gates[t][:], ALU.mult)
            return kept

        z16 = [keep.tile([P, QUARTER, PACK], BF16, name=f"z16_{v}", align_bytes=64) for v in range(U // QUARTER)]

        def write_page(t, kept):
            nc.vector.tensor_tensor(pages[t][:].indirect(n1_t[:]), kept[:], silus[t][:], ALU.add)
            for w0 in range(0, U, QUARTER):
                nc.scalar.activation(
                    z16[w0 // QUARTER][:, :, t], pages[t][:, w0 : w0 + QUARTER], ACT.Copy, scale=gs_t[:, t : t + 1]
                )

        kepts = [kept_old(t) for t in range(PACK - 1)]
        for t in range(PACK - 1):
            write_page(t, kepts[t])
        write_page(PACK - 1, kept_old(PACK - 1))

        xc_w_picked = keep.tile([P, C], I32, name=f"kept{PACK - 1}", align_bytes=64)
        nc.vector.tensor_copy(xc_w_picked[:].bitcast(U32), xw_table[:].bitcast(U32).indirect(cand_t[:]))
        xc_w = keep.tile([P, C], I32, name="xc_w", align_bytes=64)
        nc.vector.tensor_copy(
            xc_w[:].rearrange("p (t g i) -> p g t i", t=PACK, i=4),
            xc_w_picked[:].rearrange("p (g i t) -> p g t i", t=PACK, i=4),
        )

        z_w = keep.tile([P, U], I32, name="z_w", align_bytes=64)
        z_s = keep.tile([P, U], U8, name="z_s", align_bytes=64)
        for w0 in range(0, U, QUARTER):
            nc.vector.quantize_mx(
                out=z_w[:, w0 : w0 + QUARTER].bitcast(FP8X4),
                scales=z_s[:, w0 : w0 + QUARTER],
                in_=z16[w0 // QUARTER][:].rearrange("p w t -> p (w t)"),
            )

        def scores(t):
            s = keep.tile([P, U], F32, name=f"s{t}")
            pieces = ((0, 512), (512, 256), (768, 256)) if t == 0 else ((0, 512), (512, 512))
            for w0, n in pieces:
                acc = psum.tile([P, 512], F32, name="bank")
                nc.tensor.matmul_mx(
                    out=acc[:, :n],
                    lhsT=xc_w[:, P * t : P * (t + 1)].bitcast(FP8X4),
                    lhsT_scale=xc_s[:, P * t : P * (t + 1)],
                    rhs=z_w[:, w0 : w0 + n].bitcast(FP8X4),
                    rhs_scale=z_s[:, w0 : w0 + n],
                    start=True,
                    stop=True,
                )
                if t == 0 and w0 + n < U:
                    nc.vector.tensor_scalar(s[:, w0 : w0 + n], acc[:, :n], 0.0625, None, ALU.mult)
                else:
                    nc.scalar.activation(s[:, w0 : w0 + n], acc[:, :n], ACT.Copy, scale=0.0625)
            return s

        out_rows = out_0.rearrange("(p t) w -> p t w", t=PACK)
        out_words = out_1[0].rearrange("p c r -> p (c r)").bitcast(I32)
        o_s = keep.tile([P, U], U8, name="o_s", align_bytes=64)
        starts = [sum(CHUNKS[:c]) for c in range(len(CHUNKS))]
        steps = [(c, t) for c in range(len(CHUNKS)) for t in range(PACK)]
        outs = [keep.tile([P, PACK, width], F32, name=f"o{c}") for c, width in enumerate(CHUNKS)]
        outs16 = [keep.tile([P, width, PACK], BF16, name=f"o16_{c}", align_bytes=64) for c, width in enumerate(CHUNKS)]

        def entries(c):
            return slice(starts[c] // 16, (starts[c] + CHUNKS[c]) // 16)

        def fetch_other(c, t):
            other = ring.tile([P, CHUNKS[c]], F32, name="other")
            nc.vector.tensor_copy(other[:], ss[t][:].indirect(n3_t[:, entries(c)]))
            return other

        def regroup(c, piece):
            n = CHUNKS[c] // PACK
            cols = slice(piece * n, (piece + 1) * n)
            nc.scalar.copy(
                outs16[c][:, cols, :].rearrange("p (g i) t -> p g t i", i=4),
                outs[c][:, :, cols].rearrange("p t (g i) -> p g t i", i=4),
            )

        def hand_on(c):
            cols = slice(starts[c], starts[c] + CHUNKS[c])
            o_w = keep.tile([P, CHUNKS[c]], I32, name=f"o_w{c}", align_bytes=64)
            nc.vector.quantize_mx(
                out=o_w[:].bitcast(FP8X4), scales=o_s[:, cols], in_=outs16[c][:].rearrange("p w t -> p (w t)")
            )
            nc.sync.dma_start(out=out_words[:, cols], in_=o_w[:])

        ss = [scores(0), scores(1)]
        other = fetch_other(*steps[0])
        for i, (c, t) in enumerate(steps):
            cols = slice(starts[c], starts[c] + CHUNKS[c])
            sig = ring.tile([P, CHUNKS[c]], F32, name="sig")
            nc.scalar.activation(sig[:], ss[t][:].indirect(n2_t[:, entries(c)]), ACT.Sigmoid)
            if len(ss) < PACK:
                ss.append(scores(len(ss)))
            if c > 0:
                regroup(c - 1, t)
            prod = ring.tile([P, CHUNKS[c]], F32, name="prod")
            nc.vector.tensor_tensor(prod[:], ss[t][:, cols], sig[:], ALU.mult)
            next_other = fetch_other(*steps[i + 1]) if i + 1 < len(steps) else None
            nc.vector.tensor_tensor(outs[c][:, t, :], prod[:], other[:], ALU.max)
            other = next_other
            if t == PACK - 1:
                nc.sync.dma_start(out=out_rows[:, :, cols], in_=outs[c][:])
            if c > 1 and t == 0:
                hand_on(c - 2)
        last = len(CHUNKS) - 1
        nc.vector.tensor_copy(
            outs16[last][:].rearrange("p (g i) t -> p g t i", i=4),
            outs[last][:].rearrange("p t (g i) -> p g t i", i=4),
        )
        hand_on(last - 1)
        hand_on(last)

        out_scale_rows = out_2[0].bitcast(I32)
        for q in range(4):
            queue = nc.scalar if q % 2 == 0 else nc.sync
            queue.dma_start(out=out_scale_rows[4 * q : 4 * q + 4, :], in_=o_s[32 * q : 32 * q + 4, :].bitcast(I32))
